import numpy as np
import ml_dtypes


def mxq(x, axis, fmt="e4m3"):
    dtype, down = {"e4m3": (ml_dtypes.float8_e4m3fn, 7), "e5m2": (ml_dtypes.float8_e5m2, 14)}[fmt]
    v = np.moveaxis(np.asarray(x, np.float32).astype(ml_dtypes.bfloat16).astype(np.float64), axis, -1)
    blocks = v.reshape(v.shape[:-1] + (-1, 32))
    amax = np.abs(blocks).max(-1, keepdims=True)
    byte = np.maximum(np.where(amax > 0, np.frexp(amax)[1] - 1 + 127, 0) - down, 1)
    scale = np.exp2(byte - 127.0)
    codes = (blocks / scale).astype(np.float32).astype(dtype).astype(np.float64)
    return np.moveaxis((codes * scale).reshape(v.shape), -1, axis)


WIDE = False


def mx_kscale(k):
    if not WIDE:
        return np.ones(k)
    levels = np.array([10, -10, 5, -5, 0])
    if k % 512:
        return np.exp2(np.random.permutation(np.resize(levels, k // 32))).repeat(32)
    a = np.empty((k // 512, 16))
    for p in range(k // 512):
        a[p, :8] = np.random.permutation(np.resize(levels, 8))
        for g in range(8):
            far = levels[np.abs(levels - a[p, g]) >= 10]
            a[p, g + 8] = far[np.random.randint(len(far))]
    return np.exp2(a.ravel()).repeat(32)


def f64(x):
    return np.asarray(x).astype(np.float64)


def striped(idx):
    return np.tile(np.asarray(idx).reshape(-1, 16).T, (8, 1)).astype(np.uint16)


def unstriped(offs):
    return offs[:16].T.reshape(-1).astype(np.int64)


E2M1 = np.array([0.0, 0.5, 1.0, 1.5, 2.0, 3.0, 4.0, 6.0, -0.0, -0.5, -1.0, -1.5, -2.0, -3.0, -4.0, -6.0])


def pack_weight(w, fmt):
    k, n = w.shape
    w = f64(np.asarray(w, np.float32).astype(ml_dtypes.bfloat16)).reshape(k // 32, 32, n)
    amax = np.abs(w).max(1)
    if fmt == "e4m3":
        byte = np.frexp(amax)[1] - 1 + 127 - 7
    else:
        mant, ex = np.frexp(amax / 6.0)
        byte = np.where(mant > 0.5, ex, ex - 1) + 127
    byte = np.clip(np.where(amax > 0, byte, 1), 1, 254)
    scaled = (w * np.exp2(127.0 - byte)[:, None, :]).reshape(k, n).astype(np.float32)
    by_word = np.ascontiguousarray(scaled.reshape(k // 512, 128, 4, n).transpose(0, 1, 3, 2))
    if fmt == "e4m3":
        words = by_word.astype(ml_dtypes.float8_e4m3fn).view(np.uint8)
    else:
        c = by_word.astype(ml_dtypes.float4_e2m1fn).view(np.uint8) & 0xF
        words = (c[..., 0::2] | (c[..., 1::2] << 4)).reshape(k // 512, 128, 2 * n)
    return np.ascontiguousarray(words), np.ascontiguousarray(byte.astype(np.uint8).reshape(k // 512, 16, n))


def unpack_weight(words, scales, fmt):
    g, _, n = scales.shape
    words = np.ascontiguousarray(words).reshape(g, 128, n, -1)
    if fmt == "e4m3":
        vals = words.view(ml_dtypes.float8_e4m3fn).astype(np.float64)
    else:
        nib = np.empty((g, 128, n, 4), np.uint8)
        nib[..., 0::2] = words & 0xF
        nib[..., 1::2] = words >> 4
        vals = E2M1[nib]
    vals = vals * np.repeat(np.exp2(scales.astype(np.float64) - 127.0), 8, axis=1)[..., None]
    return vals.transpose(0, 1, 3, 2).reshape(g * 512, n)


D, E, T, I, G, U, Q = 512, 512, 4096, 1024, 64, 512, 128


def setup_inputs():
    n = np.random.standard_normal
    idx = np.random.permutation(T)[:I]
    idx2 = np.random.permutation(U)[:G]
    fd = mx_kscale(D)
    fe = mx_kscale(E)
    keysp = pack_weight(n((D, T)) / fd[:, None], "e4m3")
    valsp = pack_weight(n((E, T)) / fe[:, None], "e4m3")
    return {
        "query": (n((D, Q)) * 0.8 / np.sqrt(D) * fd[:, None]).astype(np.float32),
        "keys_words": keysp[0],
        "keys_scales": keysp[1],
        "ptab": (0.5 * n((Q, U)) - 4.3).astype(np.float32),
        "gout": (n((E, Q)) * 1 / np.sqrt(E) * fe[:, None]).astype(np.float32),
        "vals_words": valsp[0],
        "vals_scales": valsp[1],
        "old": (0.5 * n((Q, U))).astype(np.float32),
        "offs": striped(idx),
        "offs2": striped(idx2),
    }


def reference(query, keys_words, keys_scales, ptab, gout, vals_words, vals_scales, old, offs, offs2):
    idx = unstriped(offs)
    idx2 = unstriped(offs2)
    keysu = unpack_weight(keys_words, keys_scales, "e4m3")
    valsu = unpack_weight(vals_words, vals_scales, "e4m3")
    queryq = mxq(f64(query), 0, "e4m3")
    keysidxg = keysu[:, idx]
    a = queryq.T @ keysidxg
    p = np.exp(a - np.max(a, axis=1, keepdims=True))
    z = np.sum(p, axis=1, keepdims=True)
    goutq = mxq(f64(gout), 0, "e4m3")
    valsidxg = valsu[:, idx]
    c0 = goutq.T @ valsidxg
    s = p.reshape(Q, G, I // G).sum(axis=2) / z
    m1 = (p * c0).reshape(Q, G, I // G).sum(axis=2) / z
    tp = np.exp(f64(ptab)[:, idx2])
    dtp = m1 / np.square(1.0 + s / tp) * (-1.0) * s / np.square(tp) * (-1.0)
    gs = dtp * tp * 64.0
    gf = np.zeros((Q, U))
    gf[:, idx2] = gs
    y = f64(old) + gf
    return y

@@ -1,0 +1,162 @@
+from contextlib import ExitStack
+
+import concourse.mybir as mybir
+from concourse.masks import make_identity
+
+F32 = mybir.dt.float32
+BF16 = mybir.dt.bfloat16
+I32 = mybir.dt.int32
+U32 = mybir.dt.uint32
+U16 = mybir.dt.uint16
+U8 = mybir.dt.uint8
+FP8X4 = mybir.dt.float8_e4m3fn_x4
+ALU = mybir.AluOpType
+ACT = mybir.ActivationFunctionType
+AX = mybir.AxisListType
+
+P = 128
+T = 4096
+SLOTS = 1024
+PAGES = 64
+PAGE = 16
+U = 512
+Q = 128
+HALF = 512
+FLOPS = 2 * 2 * 512 * Q * SLOTS
+
+
+def by_quarter(bank):
+    return bank[:].rearrange("p (g a b) -> p a g b", a=4, b=4)
+
+
+def tile_attend_bpagecap_kernel(tc, query, keys_words, keys_scales, ptab, gout, vals_words, vals_scales, old, offs, offs2, out):
+    nc = tc.nc
+    with ExitStack() as ctx:
+        sb = ctx.enter_context(tc.tile_pool(name="sb", bufs=1))
+        reuse = ctx.enter_context(tc.tile_pool(name="reuse", bufs=1))
+        ps = ctx.enter_context(tc.psum_pool(name="ps", bufs=1))
+
+        slot_list = sb.tile([P, SLOTS // 16], U16, name="slot_list")
+        page_list = sb.tile([P, PAGES // 16], U16, name="page_list")
+        key_bytes = reuse.tile([P, T], U8, name="key_bytes", align_bytes=64, offset=4 * T)
+        val_bytes = reuse.tile([P, T], U8, name="val_bytes", align_bytes=64, offset=5 * T)
+        key_words = reuse.tile([P, T], I32, name="key_words", align_bytes=64, offset=0)
+        val_words = sb.tile([P, T], I32, name="val_words", align_bytes=64)
+        q_raw = sb.tile([P, 4, Q], F32, name="q_raw", tag="stage")
+        g_raw = sb.tile([P, 4, Q], F32, name="g_raw")
+        logcap = sb.tile([P, U], F32, name="logcap")
+        placed = sb.tile([P, U], F32, name="placed")
+
+        nc.vector.memset(key_bytes[:].bitcast(I32), 0)
+        nc.vector.memset(val_bytes[:].bitcast(I32), 0)
+        nc.vector.memset(placed[:], 0.0)
+        ident = sb.tile([P, P], F32, name="ident")
+        make_identity(nc, ident[:])
+        warm = sb.tile([P, 1], F32, name="warm")
+        nc.scalar.activation(warm[:], placed[:, 0:1], ACT.Exp)
+
+        nc.sync.dma_start(slot_list[:], offs)
+        nc.sync.dma_start(page_list[:], offs2)
+        ks_rows = keys_scales[0].bitcast(I32).rearrange("(b r) w -> r b w", r=4)
+        vs_rows = vals_scales[0].bitcast(I32).rearrange("(b r) w -> r b w", r=4)
+        for r in range(4):
+            nc.scalar.dma_start(key_bytes[r:P:32, :].bitcast(I32), ks_rows[r])
+        for r in range(4):
+            nc.gpsimd.dma_start(val_bytes[4 + r:P:32, :].bitcast(I32), vs_rows[r])
+        nc.sync.dma_start(q_raw[:], query.rearrange("(p j) w -> p j w", j=4))
+        nc.sync.dma_start(key_words[:], keys_words[0].rearrange("p n t -> p (n t)").bitcast(I32))
+        nc.sync.dma_start(g_raw[:], gout.rearrange("(p j) w -> p j w", j=4))
+        nc.sync.dma_start(logcap[:], ptab)
+        nc.sync.dma_start(val_words[:], vals_words[0].rearrange("p n t -> p (n t)").bitcast(I32))
+
+        q_grouped = sb.tile([P, Q, 4], BF16, name="q_grouped", align_bytes=64)
+        g_grouped = sb.tile([P, Q, 4], BF16, name="g_grouped", align_bytes=64)
+        nc.scalar.copy(q_grouped[:], q_raw[:].rearrange("p j w -> p w j"))
+        nc.scalar.copy(g_grouped[:], g_raw[:].rearrange("p j w -> p w j"))
+        before = sb.tile([P, U], F32, name="before", tag="stage")
+        nc.sync.dma_start(before[:], old)
+
+        kb = sb.tile([P, SLOTS], U8, name="kb", align_bytes=64)
+        nc.vector.tensor_copy(kb[:], key_bytes[:].indirect(slot_list[:]))
+        q_codes = sb.tile([P, Q], U32, name="q_codes", align_bytes=64)
+        q_scales = sb.tile([P, Q], U8, name="q_scales", align_bytes=64)
+        nc.vector.quantize_mx(q_codes[:].bitcast(FP8X4), q_scales[:], q_grouped[:].rearrange("p w j -> p (w j)"))
+
+        halves = range(SLOTS // HALF)
+        scores = [ps.tile([P, HALF], F32, name=f"scores{h}") for h in halves]
+        dots = [ps.tile([P, HALF], F32, name=f"dots{h}") for h in halves]
+        kw = [reuse.tile([P, HALF], U32, name=f"kw{h}", align_bytes=64, offset=4 * T + 4 * HALF * h) for h in halves]
+        vw = [reuse.tile([P, HALF], U32, name=f"vw{h}", align_bytes=64, offset=5 * T + 4 * HALF * h) for h in halves]
+        lists = [slot_list[:, h * (HALF // 16):(h + 1) * (HALF // 16)] for h in halves]
+        cols = [slice(h * HALF, (h + 1) * HALF) for h in halves]
+        pages = [slice(h * (HALF // PAGE), (h + 1) * (HALF // PAGE)) for h in halves]
+
+        for h in halves:
+            nc.vector.tensor_copy(kw[h][:], key_words[:].bitcast(U32).indirect(lists[h]))
+            nc.tensor.matmul_mx(scores[h][:], lhsT=q_codes[:].bitcast(FP8X4), lhsT_scale=q_scales[:],
+                                rhs=kw[h][:].bitcast(FP8X4), rhs_scale=kb[:, cols[h]], start=True, stop=True)
+        neg_max0 = sb.tile([P, 1], F32, name="neg_max0")
+        max1 = sb.tile([P, 1], F32, name="max1")
+        nc.vector.tensor_reduce(neg_max0[:], scores[0][:], AX.X, ALU.max, negate=True)
+        nc.vector.tensor_reduce(max1[:], scores[1][:], AX.X, ALU.max)
+        excess = sb.tile([P, 1], F32, name="excess")
+        nc.scalar.activation(excess[:], max1[:], ACT.Relu, bias=neg_max0[:])
+        neg_max = sb.tile([P, 1], F32, name="neg_max")
+        nc.scalar.activation(neg_max[:], excess[:], ACT.Identity, bias=neg_max0[:], scale=-1.0)
+
+        share_cap = sb.tile([P, 2, PAGES], F32, name="share_cap")
+        listed_logcap = reuse.tile([P, PAGES], F32, name="listed_logcap", align_bytes=64, offset=2048)
+        nc.vector.tensor_copy(listed_logcap[:], logcap[:].indirect(page_list[:]))
+        nc.scalar.activation(share_cap[:, 1, :], listed_logcap[:], ACT.Exp)
+        g_codes = reuse.tile([P, Q], U32, name="g_codes", align_bytes=64, offset=1024)
+        g_scales = reuse.tile([P, Q], U8, name="g_scales", align_bytes=64, offset=1536)
+        nc.vector.quantize_mx(g_codes[:].bitcast(FP8X4), g_scales[:], g_grouped[:].rearrange("p w j -> p (w j)"))
+        vb = [reuse.tile([P, HALF], U8, name=f"vb{h}", align_bytes=64, offset=HALF * h) for h in halves]
+        for h in halves:
+            nc.vector.tensor_copy(vb[h][:], val_bytes[:].indirect(lists[h]))
+
+        p = [sb.tile([P, 4, HALF // PAGE, 4], F32, name=f"p{h}") for h in halves]
+        half_sum = sb.tile([P, 2], F32, name="half_sum")
+        turned = ps.tile([P, 2, P], F32, name="turned")
+        for h in halves:
+            nc.scalar.activation(p[h][:], by_quarter(scores[h]), ACT.Exp, bias=neg_max[:], accum_out=half_sum[:, h:h + 1])
+            for a in range(4):
+                nc.tensor.matmul(turned[:, h, :], lhsT=p[h][:, a].rearrange("p g b -> p (g b)"), rhs=ident[:],
+                                 start=(a == 0), stop=(a == 3), is_transpose=True)
+        z = sb.tile([P, 1], F32, name="z")
+        nc.scalar.activation(z[:], half_sum[:, 0:1], ACT.Identity, bias=half_sum[:, 1:2])
+        turned_sb = sb.tile([P, 2, P], F32, name="turned_sb")
+        nc.scalar.copy(turned_sb[:], turned[:])
+        back = ps.tile([P, 2, P], F32, name="back")
+        for h in halves:
+            nc.tensor.transpose(back[:, h, :], turned_sb[:, h, :], ident[:])
+        nc.vector.tensor_reduce(share_cap[:, 0, :], back[:].rearrange("p h (g b) -> p (h g) b", b=4), AX.X, ALU.add)
+        den = sb.tile([P, PAGES], F32, name="den")
+        nc.vector.scalar_tensor_tensor(den[:], share_cap[:, 1, :], z[:], share_cap[:, 0, :], ALU.mult, ALU.add)
+        root = sb.tile([P, PAGES], F32, name="root")
+        nc.scalar.activation(root[:], den[:], ACT.Abs_reciprocal_sqrt)
+        inv = sb.tile([P, PAGES], F32, name="inv")
+        nc.scalar.activation(inv[:], root[:], ACT.Square)
+        ratios = sb.tile([P, 2, PAGES], F32, name="ratios")
+        nc.vector.tensor_tensor(ratios[:], share_cap[:], inv[:].unsqueeze(1).to_broadcast([P, 2, PAGES]), ALU.mult)
+        factor = sb.tile([P, PAGES], F32, name="factor")
+        nc.vector.scalar_tensor_tensor(factor[:], ratios[:, 0, :], 64.0, ratios[:, 1, :], ALU.mult, ALU.mult)
+
+        for h in halves:
+            nc.vector.tensor_copy(vw[h][:], val_words[:].bitcast(U32).indirect(lists[h]))
+            nc.tensor.matmul_mx(dots[h][:], lhsT=g_codes[:].bitcast(FP8X4), lhsT_scale=g_scales[:],
+                                rhs=vw[h][:].bitcast(FP8X4), rhs_scale=vb[h][4:P, :], start=True, stop=True)
+        weighted = [sb.tile([P, 4, HALF // PAGE, 4], F32, name=f"weighted{h}") for h in halves]
+        for h in halves:
+            nc.vector.tensor_tensor(weighted[h][:], by_quarter(dots[h]), p[h][:], ALU.mult)
+        moment = sb.tile([P, PAGES], F32, name="moment")
+        for h in halves:
+            nc.vector.tensor_reduce(moment[:, pages[h]], weighted[h][:].rearrange("p a g b -> p g a b"), AX.XY, ALU.add)
+        nc.vector.tensor_tensor(placed[:].indirect(page_list[:]), moment[:], factor[:], ALU.mult)
+
+        queues = [nc.sync, nc.scalar]
+        for h in halves:
+            part = slice(h * (U // 2), (h + 1) * (U // 2))
+            total = sb.tile([P, U // 2], F32, name=f"total{h}")
+            nc.vector.tensor_tensor(total[:], placed[:, part], before[:, part], ALU.add)
+            queues[h].dma_start(out[:, part], total[:])

@@ -1,7 +1,6 @@
 from contextlib import ExitStack
 
 import concourse.mybir as mybir
-from concourse.masks import make_identity
 
 F32 = mybir.dt.float32
 BF16 = mybir.dt.bfloat16
@@ -22,11 +21,17 @@ PAGE = 16
 U = 512
 Q = 128
 HALF = 512
+GAP_LIMIT = 60.0
+KEY_WORDS = 0
+CAPS = KEY_WORDS + 4 * T
+VAL_WORDS = CAPS + 4 * U
+KEY_BYTES = VAL_WORDS + 4 * T
+VAL_BYTES = KEY_BYTES + T
 FLOPS = 2 * 2 * 512 * Q * SLOTS
 
 
-def by_quarter(bank):
-    return bank[:].rearrange("p (g a b) -> p a g b", a=4, b=4)
+def by_page(tile):
+    return tile[:].rearrange("p (g j) -> p g j", j=PAGE)
 
 
 def tile_attend_bpagecap_kernel(tc, query, keys_words, keys_scales, ptab, gout, vals_words, vals_scales, old, offs, offs2, out):
@@ -36,122 +41,114 @@ def tile_attend_bpagecap_kernel(tc, query, keys_words, keys_scales, ptab, gout, 
         reuse = ctx.enter_context(tc.tile_pool(name="reuse", bufs=1))
         ps = ctx.enter_context(tc.psum_pool(name="ps", bufs=1))
 
+        def at(offset, shape, dtype, name):
+            return reuse.tile(shape, dtype, name=name, align_bytes=64, offset=offset)
+
         slot_list = sb.tile([P, SLOTS // 16], U16, name="slot_list")
         page_list = sb.tile([P, PAGES // 16], U16, name="page_list")
-        key_bytes = reuse.tile([P, T], U8, name="key_bytes", align_bytes=64, offset=4 * T)
-        val_bytes = reuse.tile([P, T], U8, name="val_bytes", align_bytes=64, offset=5 * T)
-        key_words = reuse.tile([P, T], I32, name="key_words", align_bytes=64, offset=0)
-        val_words = sb.tile([P, T], I32, name="val_words", align_bytes=64)
-        q_raw = sb.tile([P, 4, Q], F32, name="q_raw", tag="stage")
-        g_raw = sb.tile([P, 4, Q], F32, name="g_raw")
-        logcap = sb.tile([P, U], F32, name="logcap")
+        key_bytes = at(KEY_BYTES, [P, T], U8, "key_bytes")
+        val_bytes = at(VAL_BYTES, [P, T], U8, "val_bytes")
         placed = sb.tile([P, U], F32, name="placed")
 
         nc.vector.memset(key_bytes[:].bitcast(I32), 0)
         nc.vector.memset(val_bytes[:].bitcast(I32), 0)
         nc.vector.memset(placed[:], 0.0)
-        ident = sb.tile([P, P], F32, name="ident")
-        make_identity(nc, ident[:])
-        warm = sb.tile([P, 1], F32, name="warm")
-        nc.scalar.activation(warm[:], placed[:, 0:1], ACT.Exp)
 
+        q_raw = at(CAPS - 1024, [P, 4, Q], F32, "q_raw")
+        g_raw = at(VAL_WORDS, [P, 4, Q], F32, "g_raw")
+        nc.sync.dma_start(q_raw[:], query.rearrange("(p j) w -> p j w", j=4))
         nc.sync.dma_start(slot_list[:], offs)
+        nc.sync.dma_start(g_raw[:], gout.rearrange("(p j) w -> p j w", j=4))
         nc.sync.dma_start(page_list[:], offs2)
         ks_rows = keys_scales[0].bitcast(I32).rearrange("(b r) w -> r b w", r=4)
         vs_rows = vals_scales[0].bitcast(I32).rearrange("(b r) w -> r b w", r=4)
         for r in range(4):
-            nc.scalar.dma_start(key_bytes[r:P:32, :].bitcast(I32), ks_rows[r])
+            nc.sync.dma_start(key_bytes[r:P:32, :].bitcast(I32), ks_rows[r])
         for r in range(4):
-            nc.gpsimd.dma_start(val_bytes[4 + r:P:32, :].bitcast(I32), vs_rows[r])
-        nc.sync.dma_start(q_raw[:], query.rearrange("(p j) w -> p j w", j=4))
+            nc.sync.dma_start(val_bytes[4 + r:P:32, :].bitcast(I32), vs_rows[r])
+
+        grouped = sb.tile([P, 2, Q, 4], BF16, name="grouped", align_bytes=64)
+        nc.vector.tensor_copy(grouped[:, 0], q_raw[:].rearrange("p j w -> p w j"))
+        nc.scalar.copy(grouped[:, 1], g_raw[:].rearrange("p j w -> p w j"))
+        key_words = at(KEY_WORDS, [P, T], I32, "key_words")
+        logcap = at(CAPS, [P, U], F32, "logcap")
+        val_words = at(VAL_WORDS, [P, T], I32, "val_words")
         nc.sync.dma_start(key_words[:], keys_words[0].rearrange("p n t -> p (n t)").bitcast(I32))
-        nc.sync.dma_start(g_raw[:], gout.rearrange("(p j) w -> p j w", j=4))
         nc.sync.dma_start(logcap[:], ptab)
         nc.sync.dma_start(val_words[:], vals_words[0].rearrange("p n t -> p (n t)").bitcast(I32))
 
-        q_grouped = sb.tile([P, Q, 4], BF16, name="q_grouped", align_bytes=64)
-        g_grouped = sb.tile([P, Q, 4], BF16, name="g_grouped", align_bytes=64)
-        nc.scalar.copy(q_grouped[:], q_raw[:].rearrange("p j w -> p w j"))
-        nc.scalar.copy(g_grouped[:], g_raw[:].rearrange("p j w -> p w j"))
-        before = sb.tile([P, U], F32, name="before", tag="stage")
-        nc.sync.dma_start(before[:], old)
-
         kb = sb.tile([P, SLOTS], U8, name="kb", align_bytes=64)
         nc.vector.tensor_copy(kb[:], key_bytes[:].indirect(slot_list[:]))
-        q_codes = sb.tile([P, Q], U32, name="q_codes", align_bytes=64)
-        q_scales = sb.tile([P, Q], U8, name="q_scales", align_bytes=64)
-        nc.vector.quantize_mx(q_codes[:].bitcast(FP8X4), q_scales[:], q_grouped[:].rearrange("p w j -> p (w j)"))
+        row_codes = at(KEY_BYTES, [P, 2 * Q], U32, "row_codes")
+        row_scales = at(KEY_BYTES + 1024, [P, 2 * Q], U8, "row_scales")
+        nc.vector.quantize_mx(row_codes[:].bitcast(FP8X4), row_scales[:], grouped[:].rearrange("p s w j -> p (s w j)"))
+        vb = sb.tile([P, SLOTS], U8, name="vb", align_bytes=64)
+        nc.vector.tensor_copy(vb[:], val_bytes[:].indirect(slot_list[:]))
+        before = at(VAL_BYTES + 2048, [P, U], F32, "before")
+        nc.sync.dma_start(before[:], old)
 
         halves = range(SLOTS // HALF)
         scores = [ps.tile([P, HALF], F32, name=f"scores{h}") for h in halves]
         dots = [ps.tile([P, HALF], F32, name=f"dots{h}") for h in halves]
-        kw = [reuse.tile([P, HALF], U32, name=f"kw{h}", align_bytes=64, offset=4 * T + 4 * HALF * h) for h in halves]
-        vw = [reuse.tile([P, HALF], U32, name=f"vw{h}", align_bytes=64, offset=5 * T + 4 * HALF * h) for h in halves]
+        kw = [at(VAL_BYTES, [P, HALF], U32, "kw0"), sb.tile([P, HALF], U32, name="kw1", align_bytes=64)]
         lists = [slot_list[:, h * (HALF // 16):(h + 1) * (HALF // 16)] for h in halves]
         cols = [slice(h * HALF, (h + 1) * HALF) for h in halves]
         pages = [slice(h * (HALF // PAGE), (h + 1) * (HALF // PAGE)) for h in halves]
 
         for h in halves:
             nc.vector.tensor_copy(kw[h][:], key_words[:].bitcast(U32).indirect(lists[h]))
-            nc.tensor.matmul_mx(scores[h][:], lhsT=q_codes[:].bitcast(FP8X4), lhsT_scale=q_scales[:],
+            nc.tensor.matmul_mx(scores[h][:], lhsT=row_codes[:, 0:Q].bitcast(FP8X4), lhsT_scale=row_scales[:, 0:Q],
                                 rhs=kw[h][:].bitcast(FP8X4), rhs_scale=kb[:, cols[h]], start=True, stop=True)
-        neg_max0 = sb.tile([P, 1], F32, name="neg_max0")
-        max1 = sb.tile([P, 1], F32, name="max1")
-        nc.vector.tensor_reduce(neg_max0[:], scores[0][:], AX.X, ALU.max, negate=True)
-        nc.vector.tensor_reduce(max1[:], scores[1][:], AX.X, ALU.max)
-        excess = sb.tile([P, 1], F32, name="excess")
-        nc.scalar.activation(excess[:], max1[:], ACT.Relu, bias=neg_max0[:])
-        neg_max = sb.tile([P, 1], F32, name="neg_max")
-        nc.scalar.activation(neg_max[:], excess[:], ACT.Identity, bias=neg_max0[:], scale=-1.0)
-
-        share_cap = sb.tile([P, 2, PAGES], F32, name="share_cap")
-        listed_logcap = reuse.tile([P, PAGES], F32, name="listed_logcap", align_bytes=64, offset=2048)
-        nc.vector.tensor_copy(listed_logcap[:], logcap[:].indirect(page_list[:]))
-        nc.scalar.activation(share_cap[:, 1, :], listed_logcap[:], ACT.Exp)
-        g_codes = reuse.tile([P, Q], U32, name="g_codes", align_bytes=64, offset=1024)
-        g_scales = reuse.tile([P, Q], U8, name="g_scales", align_bytes=64, offset=1536)
-        nc.vector.quantize_mx(g_codes[:].bitcast(FP8X4), g_scales[:], g_grouped[:].rearrange("p w j -> p (w j)"))
-        vb = [reuse.tile([P, HALF], U8, name=f"vb{h}", align_bytes=64, offset=HALF * h) for h in halves]
-        for h in halves:
-            nc.vector.tensor_copy(vb[h][:], val_bytes[:].indirect(lists[h]))
-
-        p = [sb.tile([P, 4, HALF // PAGE, 4], F32, name=f"p{h}") for h in halves]
+        neg_max = sb.tile([P, 2], F32, name="neg_max")
+        p = [sb.tile([P, HALF], F32, name=f"p{h}") for h in halves]
         half_sum = sb.tile([P, 2], F32, name="half_sum")
-        turned = ps.tile([P, 2, P], F32, name="turned")
         for h in halves:
-            nc.scalar.activation(p[h][:], by_quarter(scores[h]), ACT.Exp, bias=neg_max[:], accum_out=half_sum[:, h:h + 1])
-            for a in range(4):
-                nc.tensor.matmul(turned[:, h, :], lhsT=p[h][:, a].rearrange("p g b -> p (g b)"), rhs=ident[:],
-                                 start=(a == 0), stop=(a == 3), is_transpose=True)
-        z = sb.tile([P, 1], F32, name="z")
-        nc.scalar.activation(z[:], half_sum[:, 0:1], ACT.Identity, bias=half_sum[:, 1:2])
-        turned_sb = sb.tile([P, 2, P], F32, name="turned_sb")
-        nc.scalar.copy(turned_sb[:], turned[:])
-        back = ps.tile([P, 2, P], F32, name="back")
+            nc.vector.tensor_reduce(neg_max[:, h:h + 1], scores[h][:], AX.X, ALU.max, negate=True)
+            nc.scalar.activation(p[h][:], scores[h][:], ACT.Exp, bias=neg_max[:, h:h + 1], accum_out=half_sum[:, h:h + 1])
+
+        listed_logcap = at(KEY_WORDS, [P, PAGES], F32, "listed_logcap")
+        nc.vector.tensor_copy(listed_logcap[:], logcap[:].indirect(page_list[:]))
+        share_cap = sb.tile([P, 2, PAGES], F32, name="share_cap")
+        nc.scalar.activation(share_cap[:, 1, :], listed_logcap[:], ACT.Exp)
+
+        gap = sb.tile([P, 2], F32, name="gap")
         for h in halves:
-            nc.tensor.transpose(back[:, h, :], turned_sb[:, h, :], ident[:])
-        nc.vector.tensor_reduce(share_cap[:, 0, :], back[:].rearrange("p h (g b) -> p (h g) b", b=4), AX.X, ALU.add)
-        den = sb.tile([P, PAGES], F32, name="den")
-        nc.vector.scalar_tensor_tensor(den[:], share_cap[:, 1, :], z[:], share_cap[:, 0, :], ALU.mult, ALU.add)
+            nc.vector.tensor_scalar(gap[:, h:h + 1], neg_max[:, h:h + 1], neg_max[:, 1 - h:2 - h], GAP_LIMIT, ALU.subtract, ALU.min)
+        other_weight = sb.tile([P, 2], F32, name="other_weight")
+        nc.scalar.activation(other_weight[:], gap[:], ACT.Exp)
+        row_sum = sb.tile([P, 2], F32, name="row_sum")
+        capped_sum = sb.tile([P, PAGES], F32, name="capped_sum")
+        for h in halves:
+            nc.scalar.activation(row_sum[:, h:h + 1], half_sum[:, 1 - h:2 - h], ACT.Identity,
+                                 scale=other_weight[:, h:h + 1], bias=half_sum[:, h:h + 1])
+            nc.scalar.activation(capped_sum[:, pages[h]], share_cap[:, 1, pages[h]], ACT.Copy, scale=row_sum[:, h:h + 1])
+        for h in halves:
+            nc.vector.tensor_reduce(share_cap[:, 0, pages[h]], by_page(p[h]), AX.X, ALU.add)
+
+        vw = [at(KEY_WORDS + 2048 * (h + 1), [P, HALF], U32, f"vw{h}") for h in halves]
+        for h in halves:
+            nc.vector.tensor_copy(vw[h][:], val_words[:].bitcast(U32).indirect(lists[h]))
+            nc.tensor.matmul_mx(dots[h][:], lhsT=row_codes[:, Q:2 * Q].bitcast(FP8X4), lhsT_scale=row_scales[:, Q:2 * Q],
+                                rhs=vw[h][:].bitcast(FP8X4), rhs_scale=vb[4:P, cols[h]], start=True, stop=True)
+
+        den = at(VAL_WORDS, [P, PAGES], F32, "den")
+        nc.vector.tensor_tensor(den[:], capped_sum[:], share_cap[:, 0, :], ALU.add)
         root = sb.tile([P, PAGES], F32, name="root")
         nc.scalar.activation(root[:], den[:], ACT.Abs_reciprocal_sqrt)
         inv = sb.tile([P, PAGES], F32, name="inv")
         nc.scalar.activation(inv[:], root[:], ACT.Square)
+
         ratios = sb.tile([P, 2, PAGES], F32, name="ratios")
         nc.vector.tensor_tensor(ratios[:], share_cap[:], inv[:].unsqueeze(1).to_broadcast([P, 2, PAGES]), ALU.mult)
         factor = sb.tile([P, PAGES], F32, name="factor")
         nc.vector.scalar_tensor_tensor(factor[:], ratios[:, 0, :], 64.0, ratios[:, 1, :], ALU.mult, ALU.mult)
 
+        weighted = [sb.tile([P, HALF], F32, name=f"weighted{h}") for h in halves]
         for h in halves:
-            nc.vector.tensor_copy(vw[h][:], val_words[:].bitcast(U32).indirect(lists[h]))
-            nc.tensor.matmul_mx(dots[h][:], lhsT=g_codes[:].bitcast(FP8X4), lhsT_scale=g_scales[:],
-                                rhs=vw[h][:].bitcast(FP8X4), rhs_scale=vb[h][4:P, :], start=True, stop=True)
-        weighted = [sb.tile([P, 4, HALF // PAGE, 4], F32, name=f"weighted{h}") for h in halves]
-        for h in halves:
-            nc.vector.tensor_tensor(weighted[h][:], by_quarter(dots[h]), p[h][:], ALU.mult)
+            nc.vector.tensor_tensor(weighted[h][:], dots[h][:], p[h][:], ALU.mult)
         moment = sb.tile([P, PAGES], F32, name="moment")
         for h in halves:
-            nc.vector.tensor_reduce(moment[:, pages[h]], weighted[h][:].rearrange("p a g b -> p g a b"), AX.XY, ALU.add)
+            nc.vector.tensor_reduce(moment[:, pages[h]], by_page(weighted[h]), AX.X, ALU.add)
         nc.vector.tensor_tensor(placed[:].indirect(page_list[:]), moment[:], factor[:], ALU.mult)
 
         queues = [nc.sync, nc.scalar]

@@ -21,9 +21,11 @@ PAGE = 16
 U = 512
 Q = 128
 HALF = 512
+SCALAR_PAGES = 20
 GAP_LIMIT = 60.0
 KEY_WORDS = 0
-CAPS = KEY_WORDS + 4 * T
+GRADS = KEY_WORDS + 4 * T
+CAPS = GRADS + 16 * Q
 VAL_WORDS = CAPS + 4 * U
 KEY_BYTES = VAL_WORDS + 4 * T
 VAL_BYTES = KEY_BYTES + T
@@ -54,11 +56,9 @@ def tile_attend_bpagecap_kernel(tc, query, keys_words, keys_scales, ptab, gout, 
         nc.vector.memset(val_bytes[:].bitcast(I32), 0)
         nc.vector.memset(placed[:], 0.0)
 
-        q_raw = at(CAPS - 1024, [P, 4, Q], F32, "q_raw")
-        g_raw = at(VAL_WORDS, [P, 4, Q], F32, "g_raw")
+        q_raw = at(GRADS - 1024, [P, 4, Q], F32, "q_raw")
         nc.sync.dma_start(q_raw[:], query.rearrange("(p j) w -> p j w", j=4))
         nc.sync.dma_start(slot_list[:], offs)
-        nc.sync.dma_start(g_raw[:], gout.rearrange("(p j) w -> p j w", j=4))
         nc.sync.dma_start(page_list[:], offs2)
         ks_rows = keys_scales[0].bitcast(I32).rearrange("(b r) w -> r b w", r=4)
         vs_rows = vals_scales[0].bitcast(I32).rearrange("(b r) w -> r b w", r=4)
@@ -67,21 +67,24 @@ def tile_attend_bpagecap_kernel(tc, query, keys_words, keys_scales, ptab, gout, 
         for r in range(4):
             nc.sync.dma_start(val_bytes[4 + r:P:32, :].bitcast(I32), vs_rows[r])
 
-        grouped = sb.tile([P, 2, Q, 4], BF16, name="grouped", align_bytes=64)
-        nc.vector.tensor_copy(grouped[:, 0], q_raw[:].rearrange("p j w -> p w j"))
-        nc.scalar.copy(grouped[:, 1], g_raw[:].rearrange("p j w -> p w j"))
+        q_grouped = at(VAL_WORDS - 512, [P, Q, 4], BF16, "q_grouped")
+        nc.vector.tensor_copy(q_grouped[:], q_raw[:].rearrange("p j w -> p w j"))
         key_words = at(KEY_WORDS, [P, T], I32, "key_words")
+        g_raw = at(GRADS, [P, 4, Q], F32, "g_raw")
+        nc.sync.dma_start(key_words[:], keys_words[0].rearrange("p n t -> p (n t)").bitcast(I32))
+        nc.sync.dma_start(g_raw[:], gout.rearrange("(p j) w -> p j w", j=4))
+        q_codes = sb.tile([P, Q], U32, name="q_codes", align_bytes=64)
+        q_scales = sb.tile([P, Q], U8, name="q_scales", align_bytes=64)
+        nc.vector.quantize_mx(q_codes[:].bitcast(FP8X4), q_scales[:], q_grouped[:].rearrange("p w j -> p (w j)"))
         logcap = at(CAPS, [P, U], F32, "logcap")
         val_words = at(VAL_WORDS, [P, T], I32, "val_words")
-        nc.sync.dma_start(key_words[:], keys_words[0].rearrange("p n t -> p (n t)").bitcast(I32))
         nc.sync.dma_start(logcap[:], ptab)
         nc.sync.dma_start(val_words[:], vals_words[0].rearrange("p n t -> p (n t)").bitcast(I32))
+        g_grouped = sb.tile([P, Q, 4], BF16, name="g_grouped", align_bytes=64)
+        nc.scalar.copy(g_grouped[:], g_raw[:].rearrange("p j w -> p w j"))
 
         kb = sb.tile([P, SLOTS], U8, name="kb", align_bytes=64)
         nc.vector.tensor_copy(kb[:], key_bytes[:].indirect(slot_list[:]))
-        row_codes = at(KEY_BYTES, [P, 2 * Q], U32, "row_codes")
-        row_scales = at(KEY_BYTES + 1024, [P, 2 * Q], U8, "row_scales")
-        nc.vector.quantize_mx(row_codes[:].bitcast(FP8X4), row_scales[:], grouped[:].rearrange("p s w j -> p (s w j)"))
         vb = sb.tile([P, SLOTS], U8, name="vb", align_bytes=64)
         nc.vector.tensor_copy(vb[:], val_bytes[:].indirect(slot_list[:]))
         before = at(VAL_BYTES + 2048, [P, U], F32, "before")
@@ -97,19 +100,26 @@ def tile_attend_bpagecap_kernel(tc, query, keys_words, keys_scales, ptab, gout, 
 
         for h in halves:
             nc.vector.tensor_copy(kw[h][:], key_words[:].bitcast(U32).indirect(lists[h]))
-            nc.tensor.matmul_mx(scores[h][:], lhsT=row_codes[:, 0:Q].bitcast(FP8X4), lhsT_scale=row_scales[:, 0:Q],
+            nc.tensor.matmul_mx(scores[h][:], lhsT=q_codes[:].bitcast(FP8X4), lhsT_scale=q_scales[:],
                                 rhs=kw[h][:].bitcast(FP8X4), rhs_scale=kb[:, cols[h]], start=True, stop=True)
         neg_max = sb.tile([P, 2], F32, name="neg_max")
-        p = [sb.tile([P, HALF], F32, name=f"p{h}") for h in halves]
+        p = [sb.tile([P, HALF], F32, name=f"p{h}", tag=f"p{h}") for h in halves]
         half_sum = sb.tile([P, 2], F32, name="half_sum")
-        for h in halves:
+
+        def exponentiate(h):
             nc.vector.tensor_reduce(neg_max[:, h:h + 1], scores[h][:], AX.X, ALU.max, negate=True)
             nc.scalar.activation(p[h][:], scores[h][:], ACT.Exp, bias=neg_max[:, h:h + 1], accum_out=half_sum[:, h:h + 1])
 
+        exponentiate(0)
+        g_codes = at(KEY_WORDS + 512, [P, Q], U32, "g_codes")
+        g_scales = at(KEY_WORDS + 1024, [P, Q], U8, "g_scales")
+        nc.vector.quantize_mx(g_codes[:].bitcast(FP8X4), g_scales[:], g_grouped[:].rearrange("p w j -> p (w j)"))
         listed_logcap = at(KEY_WORDS, [P, PAGES], F32, "listed_logcap")
         nc.vector.tensor_copy(listed_logcap[:], logcap[:].indirect(page_list[:]))
         share_cap = sb.tile([P, 2, PAGES], F32, name="share_cap")
         nc.scalar.activation(share_cap[:, 1, :], listed_logcap[:], ACT.Exp)
+
+        exponentiate(1)
 
         gap = sb.tile([P, 2], F32, name="gap")
         for h in halves:
@@ -128,7 +138,7 @@ def tile_attend_bpagecap_kernel(tc, query, keys_words, keys_scales, ptab, gout, 
         vw = [at(KEY_WORDS + 2048 * (h + 1), [P, HALF], U32, f"vw{h}") for h in halves]
         for h in halves:
             nc.vector.tensor_copy(vw[h][:], val_words[:].bitcast(U32).indirect(lists[h]))
-            nc.tensor.matmul_mx(dots[h][:], lhsT=row_codes[:, Q:2 * Q].bitcast(FP8X4), lhsT_scale=row_scales[:, Q:2 * Q],
+            nc.tensor.matmul_mx(dots[h][:], lhsT=g_codes[:].bitcast(FP8X4), lhsT_scale=g_scales[:],
                                 rhs=vw[h][:].bitcast(FP8X4), rhs_scale=vb[4:P, cols[h]], start=True, stop=True)
 
         den = at(VAL_WORDS, [P, PAGES], F32, "den")
@@ -138,17 +148,20 @@ def tile_attend_bpagecap_kernel(tc, query, keys_words, keys_scales, ptab, gout, 
         inv = sb.tile([P, PAGES], F32, name="inv")
         nc.scalar.activation(inv[:], root[:], ACT.Square)
 
-        ratios = sb.tile([P, 2, PAGES], F32, name="ratios")
+        weighted = [sb.tile([P, HALF], F32, name=f"weighted{h}") for h in halves]
+        for h in halves:
+            nc.vector.tensor_tensor(weighted[h][:], dots[h][:], p[h][:], ALU.mult)
+        ratios = sb.tile([P, 2, PAGES], F32, name="ratios", tag="p1")
         nc.vector.tensor_tensor(ratios[:], share_cap[:], inv[:].unsqueeze(1).to_broadcast([P, 2, PAGES]), ALU.mult)
         factor = sb.tile([P, PAGES], F32, name="factor")
         nc.vector.scalar_tensor_tensor(factor[:], ratios[:, 0, :], 64.0, ratios[:, 1, :], ALU.mult, ALU.mult)
 
-        weighted = [sb.tile([P, HALF], F32, name=f"weighted{h}") for h in halves]
-        for h in halves:
-            nc.vector.tensor_tensor(weighted[h][:], dots[h][:], p[h][:], ALU.mult)
         moment = sb.tile([P, PAGES], F32, name="moment")
-        for h in halves:
-            nc.vector.tensor_reduce(moment[:, pages[h]], by_page(weighted[h]), AX.X, ALU.add)
+        for g in range(SCALAR_PAGES):
+            slots = weighted[0][:, g * PAGE:(g + 1) * PAGE]
+            nc.scalar.activation(slots, slots, ACT.Copy, accum_out=moment[:, g:g + 1])
+        nc.vector.tensor_reduce(moment[:, SCALAR_PAGES:HALF // PAGE], by_page(weighted[0])[:, SCALAR_PAGES:, :], AX.X, ALU.add)
+        nc.vector.tensor_reduce(moment[:, pages[1]], by_page(weighted[1]), AX.X, ALU.add)
         nc.vector.tensor_tensor(placed[:].indirect(page_list[:]), moment[:], factor[:], ALU.mult)
 
         queues = [nc.sync, nc.scalar]

@@ -1,3 +1,4 @@
+import math
 from contextlib import ExitStack
 
 import concourse.mybir as mybir
@@ -21,7 +22,7 @@ PAGE = 16
 U = 512
 Q = 128
 HALF = 512
-SCALAR_PAGES = 20
+SCALAR_PAGES = 16
 GAP_LIMIT = 60.0
 KEY_WORDS = 0
 GRADS = KEY_WORDS + 4 * T
@@ -103,7 +104,7 @@ def tile_attend_bpagecap_kernel(tc, query, keys_words, keys_scales, ptab, gout, 
             nc.tensor.matmul_mx(scores[h][:], lhsT=q_codes[:].bitcast(FP8X4), lhsT_scale=q_scales[:],
                                 rhs=kw[h][:].bitcast(FP8X4), rhs_scale=kb[:, cols[h]], start=True, stop=True)
         neg_max = sb.tile([P, 2], F32, name="neg_max")
-        p = [sb.tile([P, HALF], F32, name=f"p{h}", tag=f"p{h}") for h in halves]
+        p = [sb.tile([P, HALF], F32, name=f"p{h}") for h in halves]
         half_sum = sb.tile([P, 2], F32, name="half_sum")
 
         def exponentiate(h):
@@ -146,15 +147,15 @@ def tile_attend_bpagecap_kernel(tc, query, keys_words, keys_scales, ptab, gout, 
         root = sb.tile([P, PAGES], F32, name="root")
         nc.scalar.activation(root[:], den[:], ACT.Abs_reciprocal_sqrt)
         inv = sb.tile([P, PAGES], F32, name="inv")
-        nc.scalar.activation(inv[:], root[:], ACT.Square)
+        nc.scalar.activation(inv[:], root[:], ACT.Square, scale=math.sqrt(8.0))
 
         weighted = [sb.tile([P, HALF], F32, name=f"weighted{h}") for h in halves]
         for h in halves:
             nc.vector.tensor_tensor(weighted[h][:], dots[h][:], p[h][:], ALU.mult)
-        ratios = sb.tile([P, 2, PAGES], F32, name="ratios", tag="p1")
-        nc.vector.tensor_tensor(ratios[:], share_cap[:], inv[:].unsqueeze(1).to_broadcast([P, 2, PAGES]), ALU.mult)
+        ratios = sb.tile([P, 2, PAGES], F32, name="ratios")
+        nc.gpsimd.tensor_tensor(ratios[:], share_cap[:], inv[:].unsqueeze(1).to_broadcast([P, 2, PAGES]), ALU.mult)
         factor = sb.tile([P, PAGES], F32, name="factor")
-        nc.vector.scalar_tensor_tensor(factor[:], ratios[:, 0, :], 64.0, ratios[:, 1, :], ALU.mult, ALU.mult)
+        nc.gpsimd.tensor_tensor(factor[:], ratios[:, 0, :], ratios[:, 1, :], ALU.mult)
 
         moment = sb.tile([P, PAGES], F32, name="moment")
         for g in range(SCALAR_PAGES):

import math
from contextlib import ExitStack

import concourse.mybir as mybir

F32 = mybir.dt.float32
BF16 = mybir.dt.bfloat16
I32 = mybir.dt.int32
U32 = mybir.dt.uint32
U16 = mybir.dt.uint16
U8 = mybir.dt.uint8
FP8X4 = mybir.dt.float8_e4m3fn_x4
ALU = mybir.AluOpType
ACT = mybir.ActivationFunctionType
AX = mybir.AxisListType

P = 128
T = 4096
SLOTS = 1024
PAGES = 64
PAGE = 16
U = 512
Q = 128
HALF = 512
SCALAR_PAGES = 16
GAP_LIMIT = 60.0
KEY_WORDS = 0
GRADS = KEY_WORDS + 4 * T
CAPS = GRADS + 16 * Q
VAL_WORDS = CAPS + 4 * U
KEY_BYTES = VAL_WORDS + 4 * T
VAL_BYTES = KEY_BYTES + T
FLOPS = 2 * 2 * 512 * Q * SLOTS


def by_page(tile):
    return tile[:].rearrange("p (g j) -> p g j", j=PAGE)


def tile_attend_bpagecap_kernel(tc, query, keys_words, keys_scales, ptab, gout, vals_words, vals_scales, old, offs, offs2, out):
    nc = tc.nc
    with ExitStack() as ctx:
        sb = ctx.enter_context(tc.tile_pool(name="sb", bufs=1))
        reuse = ctx.enter_context(tc.tile_pool(name="reuse", bufs=1))
        ps = ctx.enter_context(tc.psum_pool(name="ps", bufs=1))

        def at(offset, shape, dtype, name):
            return reuse.tile(shape, dtype, name=name, align_bytes=64, offset=offset)

        slot_list = sb.tile([P, SLOTS // 16], U16, name="slot_list")
        page_list = sb.tile([P, PAGES // 16], U16, name="page_list")
        key_bytes = at(KEY_BYTES, [P, T], U8, "key_bytes")
        val_bytes = at(VAL_BYTES, [P, T], U8, "val_bytes")
        placed = sb.tile([P, U], F32, name="placed")

        nc.vector.memset(key_bytes[:].bitcast(I32), 0)
        nc.vector.memset(val_bytes[:].bitcast(I32), 0)
        nc.vector.memset(placed[:], 0.0)

        q_raw = at(GRADS - 1024, [P, 4, Q], F32, "q_raw")
        nc.sync.dma_start(q_raw[:], query.rearrange("(p j) w -> p j w", j=4))
        nc.sync.dma_start(slot_list[:], offs)
        nc.sync.dma_start(page_list[:], offs2)
        ks_rows = keys_scales[0].bitcast(I32).rearrange("(b r) w -> r b w", r=4)
        vs_rows = vals_scales[0].bitcast(I32).rearrange("(b r) w -> r b w", r=4)
        for r in range(4):
            nc.sync.dma_start(key_bytes[r:P:32, :].bitcast(I32), ks_rows[r])
        for r in range(4):
            nc.sync.dma_start(val_bytes[4 + r:P:32, :].bitcast(I32), vs_rows[r])

        q_grouped = at(VAL_WORDS - 512, [P, Q, 4], BF16, "q_grouped")
        nc.vector.tensor_copy(q_grouped[:], q_raw[:].rearrange("p j w -> p w j"))
        key_words = at(KEY_WORDS, [P, T], I32, "key_words")
        g_raw = at(GRADS, [P, 4, Q], F32, "g_raw")
        nc.sync.dma_start(key_words[:], keys_words[0].rearrange("p n t -> p (n t)").bitcast(I32))
        nc.sync.dma_start(g_raw[:], gout.rearrange("(p j) w -> p j w", j=4))
        q_codes = sb.tile([P, Q], U32, name="q_codes", align_bytes=64)
        q_scales = sb.tile([P, Q], U8, name="q_scales", align_bytes=64)
        nc.vector.quantize_mx(q_codes[:].bitcast(FP8X4), q_scales[:], q_grouped[:].rearrange("p w j -> p (w j)"))
        logcap = at(CAPS, [P, U], F32, "logcap")
        val_words = at(VAL_WORDS, [P, T], I32, "val_words")
        nc.sync.dma_start(logcap[:], ptab)
        nc.sync.dma_start(val_words[:], vals_words[0].rearrange("p n t -> p (n t)").bitcast(I32))
        g_grouped = sb.tile([P, Q, 4], BF16, name="g_grouped", align_bytes=64)
        nc.scalar.copy(g_grouped[:], g_raw[:].rearrange("p j w -> p w j"))

        kb = sb.tile([P, SLOTS], U8, name="kb", align_bytes=64)
        nc.vector.tensor_copy(kb[:], key_bytes[:].indirect(slot_list[:]))
        vb = sb.tile([P, SLOTS], U8, name="vb", align_bytes=64)
        nc.vector.tensor_copy(vb[:], val_bytes[:].indirect(slot_list[:]))
        before = at(VAL_BYTES + 2048, [P, U], F32, "before")
        nc.sync.dma_start(before[:], old)

        halves = range(SLOTS // HALF)
        scores = [ps.tile([P, HALF], F32, name=f"scores{h}") for h in halves]
        dots = [ps.tile([P, HALF], F32, name=f"dots{h}") for h in halves]
        kw = [at(VAL_BYTES, [P, HALF], U32, "kw0"), sb.tile([P, HALF], U32, name="kw1", align_bytes=64)]
        lists = [slot_list[:, h * (HALF // 16):(h + 1) * (HALF // 16)] for h in halves]
        cols = [slice(h * HALF, (h + 1) * HALF) for h in halves]
        pages = [slice(h * (HALF // PAGE), (h + 1) * (HALF // PAGE)) for h in halves]

        for h in halves:
            nc.vector.tensor_copy(kw[h][:], key_words[:].bitcast(U32).indirect(lists[h]))
            nc.tensor.matmul_mx(scores[h][:], lhsT=q_codes[:].bitcast(FP8X4), lhsT_scale=q_scales[:],
                                rhs=kw[h][:].bitcast(FP8X4), rhs_scale=kb[:, cols[h]], start=True, stop=True)
        neg_max = sb.tile([P, 2], F32, name="neg_max")
        p = [sb.tile([P, HALF], F32, name=f"p{h}") for h in halves]
        half_sum = sb.tile([P, 2], F32, name="half_sum")

        def exponentiate(h):
            nc.vector.tensor_reduce(neg_max[:, h:h + 1], scores[h][:], AX.X, ALU.max, negate=True)
            nc.scalar.activation(p[h][:], scores[h][:], ACT.Exp, bias=neg_max[:, h:h + 1], accum_out=half_sum[:, h:h + 1])

        exponentiate(0)
        g_codes = at(KEY_WORDS + 512, [P, Q], U32, "g_codes")
        g_scales = at(KEY_WORDS + 1024, [P, Q], U8, "g_scales")
        nc.vector.quantize_mx(g_codes[:].bitcast(FP8X4), g_scales[:], g_grouped[:].rearrange("p w j -> p (w j)"))
        listed_logcap = at(KEY_WORDS, [P, PAGES], F32, "listed_logcap")
        nc.vector.tensor_copy(listed_logcap[:], logcap[:].indirect(page_list[:]))
        share_cap = sb.tile([P, 2, PAGES], F32, name="share_cap")
        nc.scalar.activation(share_cap[:, 1, :], listed_logcap[:], ACT.Exp)

        exponentiate(1)

        gap = sb.tile([P, 2], F32, name="gap")
        for h in halves:
            nc.vector.tensor_scalar(gap[:, h:h + 1], neg_max[:, h:h + 1], neg_max[:, 1 - h:2 - h], GAP_LIMIT, ALU.subtract, ALU.min)
        other_weight = sb.tile([P, 2], F32, name="other_weight")
        nc.scalar.activation(other_weight[:], gap[:], ACT.Exp)
        row_sum = sb.tile([P, 2], F32, name="row_sum")
        capped_sum = sb.tile([P, PAGES], F32, name="capped_sum")
        for h in halves:
            nc.scalar.activation(row_sum[:, h:h + 1], half_sum[:, 1 - h:2 - h], ACT.Identity,
                                 scale=other_weight[:, h:h + 1], bias=half_sum[:, h:h + 1])
            nc.scalar.activation(capped_sum[:, pages[h]], share_cap[:, 1, pages[h]], ACT.Copy, scale=row_sum[:, h:h + 1])
        for h in halves:
            nc.vector.tensor_reduce(share_cap[:, 0, pages[h]], by_page(p[h]), AX.X, ALU.add)

        vw = [at(KEY_WORDS + 2048 * (h + 1), [P, HALF], U32, f"vw{h}") for h in halves]
        for h in halves:
            nc.vector.tensor_copy(vw[h][:], val_words[:].bitcast(U32).indirect(lists[h]))
            nc.tensor.matmul_mx(dots[h][:], lhsT=g_codes[:].bitcast(FP8X4), lhsT_scale=g_scales[:],
                                rhs=vw[h][:].bitcast(FP8X4), rhs_scale=vb[4:P, cols[h]], start=True, stop=True)

        den = at(VAL_WORDS, [P, PAGES], F32, "den")
        nc.vector.tensor_tensor(den[:], capped_sum[:], share_cap[:, 0, :], ALU.add)
        root = sb.tile([P, PAGES], F32, name="root")
        nc.scalar.activation(root[:], den[:], ACT.Abs_reciprocal_sqrt)
        inv = sb.tile([P, PAGES], F32, name="inv")
        nc.scalar.activation(inv[:], root[:], ACT.Square, scale=math.sqrt(8.0))

        weighted = [sb.tile([P, HALF], F32, name=f"weighted{h}") for h in halves]
        for h in halves:
            nc.vector.tensor_tensor(weighted[h][:], dots[h][:], p[h][:], ALU.mult)
        ratios = sb.tile([P, 2, PAGES], F32, name="ratios")
        nc.gpsimd.tensor_tensor(ratios[:], share_cap[:], inv[:].unsqueeze(1).to_broadcast([P, 2, PAGES]), ALU.mult)
        factor = sb.tile([P, PAGES], F32, name="factor")
        nc.gpsimd.tensor_tensor(factor[:], ratios[:, 0, :], ratios[:, 1, :], ALU.mult)

        moment = sb.tile([P, PAGES], F32, name="moment")
        for g in range(SCALAR_PAGES):
            slots = weighted[0][:, g * PAGE:(g + 1) * PAGE]
            nc.scalar.activation(slots, slots, ACT.Copy, accum_out=moment[:, g:g + 1])
        nc.vector.tensor_reduce(moment[:, SCALAR_PAGES:HALF // PAGE], by_page(weighted[0])[:, SCALAR_PAGES:, :], AX.X, ALU.add)
        nc.vector.tensor_reduce(moment[:, pages[1]], by_page(weighted[1]), AX.X, ALU.add)
        nc.vector.tensor_tensor(placed[:].indirect(page_list[:]), moment[:], factor[:], ALU.mult)

        queues = [nc.sync, nc.scalar]
        for h in halves:
            part = slice(h * (U // 2), (h + 1) * (U // 2))
            total = sb.tile([P, U // 2], F32, name=f"total{h}")
            nc.vector.tensor_tensor(total[:], placed[:, part], before[:, part], ALU.add)
            queues[h].dma_start(out[:, part], total[:])
